import numpy as np
import ml_dtypes


def mxq(x, axis, fmt="e4m3"):
    dtype, down = {"e4m3": (ml_dtypes.float8_e4m3fn, 7), "e5m2": (ml_dtypes.float8_e5m2, 14)}[fmt]
    v = np.moveaxis(np.asarray(x, np.float32).astype(ml_dtypes.bfloat16).astype(np.float64), axis, -1)
    blocks = v.reshape(v.shape[:-1] + (-1, 32))
    amax = np.abs(blocks).max(-1, keepdims=True)
    byte = np.maximum(np.where(amax > 0, np.frexp(amax)[1] - 1 + 127, 0) - down, 1)
    scale = np.exp2(byte - 127.0)
    codes = (blocks / scale).astype(np.float32).astype(dtype).astype(np.float64)
    return np.moveaxis((codes * scale).reshape(v.shape), -1, axis)


WIDE = False


def mx_kscale(k):
    if not WIDE:
        return np.ones(k)
    levels = np.array([10, -10, 5, -5, 0])
    if k % 512:
        return np.exp2(np.random.permutation(np.resize(levels, k // 32))).repeat(32)
    a = np.empty((k // 512, 16))
    for p in range(k // 512):
        a[p, :8] = np.random.permutation(np.resize(levels, 8))
        for g in range(8):
            far = levels[np.abs(levels - a[p, g]) >= 10]
            a[p, g + 8] = far[np.random.randint(len(far))]
    return np.exp2(a.ravel()).repeat(32)


def f64(x):
    return np.asarray(x).astype(np.float64)


def striped(idx):
    return np.tile(np.asarray(idx).reshape(-1, 16).T, (8, 1)).astype(np.uint16)


def unstriped(offs):
    return offs[:16].T.reshape(-1).astype(np.int64)


def striped8(idx):
    return np.asarray(idx).reshape(8, -1, 16).transpose(0, 2, 1).reshape(128, -1).astype(np.uint16)


def unstriped8(offs):
    return offs.reshape(8, 16, -1).transpose(0, 2, 1).reshape(8, -1).astype(np.int64)


def pick8(x, idx, run):
    r = np.arange(len(x))
    return x[r[:, None], idx[r % (8 * run) // run]]


E2M1 = np.array([0.0, 0.5, 1.0, 1.5, 2.0, 3.0, 4.0, 6.0, -0.0, -0.5, -1.0, -1.5, -2.0, -3.0, -4.0, -6.0])


def pack_weight(w, fmt):
    k, n = w.shape
    w = f64(np.asarray(w, np.float32).astype(ml_dtypes.bfloat16)).reshape(k // 32, 32, n)
    amax = np.abs(w).max(1)
    if fmt == "e4m3":
        byte = np.frexp(amax)[1] - 1 + 127 - 7
    else:
        mant, ex = np.frexp(amax / 6.0)
        byte = np.where(mant > 0.5, ex, ex - 1) + 127
    byte = np.clip(np.where(amax > 0, byte, 1), 1, 254)
    scaled = (w * np.exp2(127.0 - byte)[:, None, :]).reshape(k, n).astype(np.float32)
    by_word = np.ascontiguousarray(scaled.reshape(k // 512, 128, 4, n).transpose(0, 1, 3, 2))
    if fmt == "e4m3":
        words = by_word.astype(ml_dtypes.float8_e4m3fn).view(np.uint8)
    else:
        c = by_word.astype(ml_dtypes.float4_e2m1fn).view(np.uint8) & 0xF
        words = (c[..., 0::2] | (c[..., 1::2] << 4)).reshape(k // 512, 128, 2 * n)
    return np.ascontiguousarray(words), np.ascontiguousarray(byte.astype(np.uint8).reshape(k // 512, 16, n))


def unpack_weight(words, scales, fmt):
    g, _, n = scales.shape
    words = np.ascontiguousarray(words).reshape(g, 128, n, -1)
    if fmt == "e4m3":
        vals = words.view(ml_dtypes.float8_e4m3fn).astype(np.float64)
    else:
        nib = np.empty((g, 128, n, 4), np.uint8)
        nib[..., 0::2] = words & 0xF
        nib[..., 1::2] = words >> 4
        vals = E2M1[nib]
    vals = vals * np.repeat(np.exp2(scales.astype(np.float64) - 127.0), 8, axis=1)[..., None]
    return vals.transpose(0, 1, 3, 2).reshape(g * 512, n)


K, J, R, T, U, Z, M, O, D, N = 512, 256, 512, 1024, 512, 512, 1024, 128, 512, 256


def setup_inputs():
    n = np.random.standard_normal
    idx = np.stack([np.random.permutation(T)[:J] for _ in range(8)])
    idx2 = np.stack([np.random.permutation(U)[:J] for _ in range(8)])
    idx3 = np.stack([np.random.permutation(U)[:J] for _ in range(8)])
    idx4 = np.random.permutation(M)[:J]
    idx5 = np.stack([np.random.permutation(J)[:O] for _ in range(8)])
    idx6 = np.stack([np.random.permutation(D)[:O] for _ in range(8)])
    idx7 = np.stack([np.random.permutation(D)[:O] for _ in range(8)])
    fk = mx_kscale(K)
    fr = mx_kscale(R)
    fz = mx_kscale(Z)
    wp = pack_weight(n((K, R)) * 1 / np.sqrt(K) / fk[:, None] * fr, "e4m3")
    xop = pack_weight(n((Z, M)) / fz[:, None], "e4m3")
    w2p = pack_weight(n((Z, R)) * 1 / np.sqrt(Z) * fz[:, None] * fr, "e2m1")
    wbp = pack_weight(n((R, N)) * 1 / np.sqrt(R) / fr[:, None], "e2m1")
    return {
        "ta": (np.random.randint(-7, 8, (K, T)).astype(np.float64)).astype(np.float32),
        "ga": ((np.random.randint(8, 25, (K, 1)) / 64.0) * fk[:, None]).astype(np.float32),
        "gb": (np.random.uniform(0.5, 1.6, (K, 1))).astype(np.float32),
        "w_words": wp[0],
        "w_scales": wp[1],
        "xo_words": xop[0],
        "xo_scales": xop[1],
        "w2_words": w2p[0],
        "w2_scales": w2p[1],
        "tl": (np.random.randint(-7, 8, (R, D)).astype(np.float64)).astype(np.float32),
        "sa": (np.random.uniform(0.5, 1.6, (R, 1))).astype(np.float32),
        "sl": ((np.random.randint(6, 19, (R, 1)) / 64.0) * fr[:, None]).astype(np.float32),
        "sm": ((np.random.randint(4, 15, (R, 1)) / 64.0) * fr[:, None]).astype(np.float32),
        "wb_words": wbp[0],
        "wb_scales": wbp[1],
        "offs": striped8(idx),
        "offs2": striped8(idx2),
        "offs3": striped8(idx3),
        "offs4": striped(idx4),
        "offs5": striped8(idx5),
        "offs6": striped8(idx6),
        "offs7": striped8(idx7),
    }


def reference(ta, ga, gb, w_words, w_scales, xo_words, xo_scales, w2_words, w2_scales, tl, sa, sl, sm, wb_words, wb_scales, offs, offs2, offs3, offs4, offs5, offs6, offs7):
    idx = unstriped8(offs)
    idx2 = unstriped8(offs2)
    idx3 = unstriped8(offs3)
    idx4 = unstriped(offs4)
    idx5 = unstriped8(offs5)
    idx6 = unstriped8(offs6)
    idx7 = unstriped8(offs7)
    wu = unpack_weight(w_words, w_scales, "e4m3")
    xou = unpack_weight(xo_words, xo_scales, "e4m3")
    w2u = unpack_weight(w2_words, w2_scales, "e2m1")
    wbu = unpack_weight(wb_words, wb_scales, "e2m1")
    xcd = pick8(f64(ta), idx, 64) * f64(ga)
    xcp = np.zeros((K, U))
    xcp[np.arange(K)[:, None], idx2[np.arange(K) % 512 // 64]] = xcd
    xc = pick8(xcp, idx3, 64) * f64(gb)
    xcq = mxq(xc, 0, "e4m3")
    xoidx4g = xou[:, idx4]
    a = wu.T @ xcq + w2u.T @ xoidx4g
    hid = np.maximum(np.minimum(pick8(a, idx5, 64) * f64(sa), pick8(f64(tl), idx6, 64) * f64(sl)), pick8(f64(tl), idx7, 64) * f64(sm))
    hidq = mxq(hid, 0, "e4m3")
    y = wbu.T @ hidq
    return y

@@ -1,0 +1,225 @@
+from contextlib import ExitStack
+
+import concourse.mybir as mybir
+
+K, J, R, T, U, Z, M, O, D, N = 512, 256, 512, 1024, 512, 512, 1024, 128, 512, 256
+FLOPS = 2 * (K * R * J + Z * R * J + R * N * O)
+
+F32 = mybir.dt.float32
+BF16 = mybir.dt.bfloat16
+I32 = mybir.dt.int32
+U32 = mybir.dt.uint32
+U16 = mybir.dt.uint16
+U8 = mybir.dt.uint8
+FP8X4 = mybir.dt.float8_e4m3fn_x4
+FP4X4 = mybir.dt.float4_e2m1fn_x4
+COPY = mybir.ActivationFunctionType.Copy
+ALU = mybir.AluOpType
+
+P = 128
+PACK = 4
+QUAD = 32
+
+
+def tile_picked_codepage_plain_bank_codedbounds_one_plain_kernel(
+    tc, ta, ga, gb, w_words, w_scales, xo_words, xo_scales, w2_words, w2_scales, tl, sa, sl, sm,
+    wb_words, wb_scales, offs, offs2, offs3, offs4, offs5, offs6, offs7, out,
+):
+    nc = tc.nc
+    with ExitStack() as ctx:
+        keep = ctx.enter_context(tc.tile_pool(name="keep", bufs=1))
+        psum = ctx.enter_context(tc.psum_pool(name="psum", bufs=1))
+
+        def load_list(src, name):
+            tile = keep.tile(list(src.shape), U16, name=name)
+            nc.sync.dma_start(tile[:], src)
+            return tile
+
+        def load_factors(queue, src, name):
+            tile = keep.tile([P, PACK], F32, name=name)
+            queue.dma_start(tile[:], src.rearrange("(p t) o -> p (t o)", t=PACK))
+            return tile
+
+        def load_plane(src, t, name):
+            tile = keep.tile([P, src.shape[1]], F32, name=name, align_bytes=64)
+            nc.sync.dma_start(tile[:], src.rearrange("(p t) c -> p t c", t=PACK)[:, t, :])
+            return tile
+
+        def load_words(src, name):
+            words = src.bitcast(I32)
+            tile = keep.tile([P, words.shape[1]], I32, name=name, align_bytes=64)
+            nc.sync.dma_start(tile[:], words)
+            return tile
+
+        def load_scale_rows(queue, tile, src, first):
+            rows = src[0].bitcast(I32)
+            for q in range(4):
+                p0 = QUAD * q + first
+                queue.dma_start(tile[p0 : p0 + 4, :].bitcast(I32), rows[4 * q : 4 * q + 4, :])
+
+        pages = [keep.tile([P, U], F32, name="page%d" % t) for t in range(PACK)]
+        xo_sc = keep.tile([P, M], U8, align_bytes=64)
+        RW = R // 4
+        spread = keep.tile([P, 2 * RW], I32, align_bytes=64)
+        wb_sc = keep.tile([P, N], U8, align_bytes=64)
+        staged = keep.tile([PACK, PACK, 2 * RW], I32)
+        for src, c0 in ((w2_scales, 0), (w_scales, RW)):
+            rows = src[0].bitcast(I32).rearrange("(q i) c -> i q c", i=PACK)
+            nc.scalar.dma_start(staged[:, :, c0 : c0 + RW], rows)
+        warm = keep.tile([P, 2], F32)
+        nc.vector.memset(warm[:, 0:1], 0.0)
+        nc.scalar.activation(out=warm[:, 1:2], in_=warm[:, 0:1], func=COPY)
+        nc.gpsimd.memset(wb_sc[:].bitcast(I32), 0)
+        nc.vector.memset(spread[:], 0)
+        nc.vector.memset(xo_sc[:].bitcast(I32), 0)
+        for t in range(PACK):
+            nc.vector.memset(pages[t][:], 0.0)
+
+        sl_t = load_factors(nc.gpsimd, sl, "sl_t")
+        sm_t = load_factors(nc.gpsimd, sm, "sm_t")
+        load_scale_rows(nc.gpsimd, wb_sc, wb_scales, 0)
+        for q in range(4):
+            nc.vector.tensor_copy(spread[QUAD * q : QUAD * q + 4, :], staged[:, q, :])
+        sc_dealt = keep.tile([P, 2 * R], U8, align_bytes=64)
+        nc.gpsimd.tensor_copy(
+            sc_dealt[:].rearrange("p (w t c i) -> p w c t i", w=2, t=PACK, i=16),
+            spread[:].bitcast(U8).rearrange("p (w c i t) -> p w c t i", w=2, t=PACK, i=16),
+        )
+
+        ta_t = [load_plane(ta, 0, "ta0")]
+        l1 = load_list(offs, "l1")
+        ga_t = load_factors(nc.sync, ga, "ga_t")
+        l2 = load_list(offs2, "l2")
+        ta_t.append(load_plane(ta, 1, "ta1"))
+        w2_raw = load_words(w2_words[0], "w2_raw")
+        w_raw = load_words(w_words[0].rearrange("p n t -> p (n t)"), "w_raw")
+        ta_t.append(load_plane(ta, 2, "ta2"))
+        l6 = load_list(offs6, "l6")
+        l7 = load_list(offs7, "l7")
+        tl_t = [load_plane(tl, 0, "tl0")]
+        ta_t.append(load_plane(ta, 3, "ta3"))
+        l3 = load_list(offs3, "l3")
+        gb_t = load_factors(nc.sync, gb, "gb_t")
+        tl_t.append(load_plane(tl, 1, "tl1"))
+        l4 = load_list(offs4, "l4")
+        load_scale_rows(nc.sync, xo_sc, xo_scales, 0)
+        xo_w = load_words(xo_words[0].rearrange("p n t -> p (n t)"), "xo_w")
+        for t in range(2, PACK):
+            tl_t.append(load_plane(tl, t, "tl%d" % t))
+        l5 = load_list(offs5, "l5")
+        sa_t = load_factors(nc.sync, sa, "sa_t")
+        wb_w = load_words(wb_words[0], "wb_w")
+
+        w2_dealt = keep.tile([P, 2 * R], U8, align_bytes=64)
+        w_dealt = keep.tile([P, R], U32, align_bytes=64)
+
+        xcd = [keep.tile([P, J], F32, name="xcd%d" % t) for t in range(PACK)]
+        for t in range(PACK):
+            nc.scalar.activation(out=xcd[t][:], in_=ta_t[t][:].indirect(l1[:]), func=COPY, scale=ga_t[:, t : t + 1])
+            nc.vector.tensor_copy(pages[t][:].indirect(l2[:]), xcd[t][:])
+            if t == 1:
+                nc.scalar.copy(
+                    w2_dealt[:].bitcast(U16).rearrange("p (t c i) -> p c t i", t=PACK, i=8),
+                    w2_raw[:].bitcast(U16).rearrange("p (c i t) -> p c t i", t=PACK, i=8),
+                )
+                nc.scalar.copy(
+                    w_dealt[:].rearrange("p (t c i) -> p c t i", t=PACK, i=4),
+                    w_raw[:].bitcast(U32).rearrange("p (c i t) -> p c t i", t=PACK, i=4),
+                )
+
+        upper = keep.tile([P, PACK, O], F32)
+        lower = keep.tile([P, PACK, O], F32)
+
+        def bounds(t):
+            nc.scalar.activation(out=upper[:, t, :], in_=tl_t[t][:].indirect(l6[:]), func=COPY, scale=sl_t[:, t : t + 1])
+            nc.scalar.activation(out=lower[:, t, :], in_=tl_t[t][:].indirect(l7[:]), func=COPY, scale=sm_t[:, t : t + 1])
+
+        bounds(0)
+        xc_planes = keep.tile([P, PACK, J], BF16, tag="ta3", align_bytes=64)
+
+        def read_page(t):
+            nc.scalar.activation(out=xc_planes[:, t, :], in_=pages[t][:].indirect(l3[:]), func=COPY, scale=gb_t[:, t : t + 1])
+
+        read_page(0)
+        read_page(1)
+        bounds(1)
+        read_page(2)
+        read_page(3)
+        bounds(2)
+        bounds(3)
+
+        xo_gw = keep.tile([P, J], U32, align_bytes=64)
+        xo_gs = keep.tile([P, J], U8, align_bytes=64)
+        nc.vector.tensor_copy(xo_gw[:], xo_w[:].bitcast(U32).indirect(l4[:]))
+        nc.vector.tensor_copy(xo_gs[:], xo_sc[:].indirect(l4[:]))
+
+        xc_in = keep.tile([P, J, PACK], BF16, tag="xo_w", align_bytes=64)
+        nc.vector.tensor_copy(
+            xc_in[:].rearrange("p (c i) t -> p c t i", i=4),
+            xc_planes[:].rearrange("p t (c i) -> p c t i", i=4),
+        )
+
+        xc_w = keep.tile([P, J], U32, align_bytes=64)
+        xc_s = keep.tile([P, J], U8, align_bytes=64)
+        nc.vector.quantize_mx(out=xc_w[:].bitcast(FP8X4), scales=xc_s[:], in_=xc_in[:].rearrange("p j t -> p (j t)"))
+
+        banks = [psum.tile([P, J], F32, name="bank%d" % t) for t in range(PACK)]
+        for t in range(PACK):
+            nc.tensor.matmul_mx(
+                out=banks[t][:],
+                lhsT=w2_dealt[:, 2 * P * t : 2 * P * (t + 1)].bitcast(FP4X4),
+                lhsT_scale=sc_dealt[:, P * t : P * (t + 1)],
+                rhs=xo_gw[:].bitcast(FP8X4),
+                rhs_scale=xo_gs[:],
+                start=True,
+                stop=False,
+            )
+        for t in range(PACK):
+            nc.tensor.matmul_mx(
+                out=banks[t][:],
+                lhsT=w_dealt[:, P * t : P * (t + 1)].bitcast(FP8X4),
+                lhsT_scale=sc_dealt[:, R + P * t : R + P * (t + 1)],
+                rhs=xc_w[:].bitcast(FP8X4),
+                rhs_scale=xc_s[:],
+                start=False,
+                stop=True,
+            )
+
+        a_t = [keep.tile([P, J], F32, name="a%d" % t) for t in range(PACK)]
+        picked = keep.tile([P, PACK, O], F32)
+        capped = keep.tile([P, PACK, O], F32)
+        for t in range(PACK):
+            nc.vector.tensor_copy(a_t[t][:], banks[t][:])
+        for t in range(PACK):
+            nc.scalar.activation(out=picked[:, t, :], in_=a_t[t][:].indirect(l5[:]), func=COPY, scale=sa_t[:, t : t + 1])
+            nc.vector.tensor_tensor(capped[:, t, :], picked[:, t, :], upper[:, t, :], ALU.min)
+        hid_in = keep.tile([P, O, PACK], BF16, align_bytes=64)
+        nc.vector.tensor_tensor(
+            hid_in[:].rearrange("p (c i) t -> p c t i", i=4),
+            capped[:].rearrange("p t (c i) -> p c t i", i=4),
+            lower[:].rearrange("p t (c i) -> p c t i", i=4),
+            ALU.max,
+        )
+        hid_w = keep.tile([P, O], U32, align_bytes=64)
+        hid_s = keep.tile([P, O], U8, align_bytes=64)
+        nc.vector.quantize_mx(out=hid_w[:].bitcast(FP8X4), scales=hid_s[:], in_=hid_in[:].rearrange("p o t -> p (o t)"))
+
+        wb_bytes = wb_w[:].bitcast(U8)
+        for h in range(N // P):
+            acc = psum.tile([P, O], F32, name="acc%d" % h)
+            nc.tensor.matmul_mx(
+                out=acc[:],
+                lhsT=wb_bytes[:, 2 * P * h : 2 * P * (h + 1)].bitcast(FP4X4),
+                lhsT_scale=wb_sc[:, P * h : P * (h + 1)],
+                rhs=hid_w[:].bitcast(FP8X4),
+                rhs_scale=hid_s[:],
+                start=True,
+                stop=True,
+            )
+            res = keep.tile([P, O], F32, name="res%d" % h)
+            if h == 0:
+                nc.vector.tensor_copy(res[:], acc[:])
+                nc.sync.dma_start(out[P * h : P * (h + 1), :], res[:])
+            else:
+                nc.scalar.copy(res[:], acc[:])
+                nc.scalar.dma_start(out[P * h : P * (h + 1), :], res[:])

@@ -65,23 +65,23 @@ def tile_picked_codepage_plain_bank_codedbounds_one_plain_kernel(
         staged = keep.tile([PACK, PACK, 2 * RW], I32)
         for src, c0 in ((w2_scales, 0), (w_scales, RW)):
             rows = src[0].bitcast(I32).rearrange("(q i) c -> i q c", i=PACK)
-            nc.scalar.dma_start(staged[:, :, c0 : c0 + RW], rows)
+            nc.sync.dma_start(staged[:, :, c0 : c0 + RW], rows)
         warm = keep.tile([P, 2], F32)
         nc.vector.memset(warm[:, 0:1], 0.0)
         nc.scalar.activation(out=warm[:, 1:2], in_=warm[:, 0:1], func=COPY)
+        nc.gpsimd.memset(xo_sc[:].bitcast(I32), 0)
+        load_scale_rows(nc.gpsimd, xo_sc, xo_scales, 0)
         nc.gpsimd.memset(wb_sc[:].bitcast(I32), 0)
         nc.vector.memset(spread[:], 0)
-        nc.vector.memset(xo_sc[:].bitcast(I32), 0)
         for t in range(PACK):
             nc.vector.memset(pages[t][:], 0.0)
 
-        sl_t = load_factors(nc.gpsimd, sl, "sl_t")
-        sm_t = load_factors(nc.gpsimd, sm, "sm_t")
+        sa_t = load_factors(nc.gpsimd, sa, "sa_t")
         load_scale_rows(nc.gpsimd, wb_sc, wb_scales, 0)
         for q in range(4):
             nc.vector.tensor_copy(spread[QUAD * q : QUAD * q + 4, :], staged[:, q, :])
         sc_dealt = keep.tile([P, 2 * R], U8, align_bytes=64)
-        nc.gpsimd.tensor_copy(
+        nc.vector.tensor_copy(
             sc_dealt[:].rearrange("p (w t c i) -> p w c t i", w=2, t=PACK, i=16),
             spread[:].bitcast(U8).rearrange("p (w c i t) -> p w c t i", w=2, t=PACK, i=16),
         )
@@ -94,20 +94,20 @@ def tile_picked_codepage_plain_bank_codedbounds_one_plain_kernel(
         w2_raw = load_words(w2_words[0], "w2_raw")
         w_raw = load_words(w_words[0].rearrange("p n t -> p (n t)"), "w_raw")
         ta_t.append(load_plane(ta, 2, "ta2"))
+        ta_t.append(load_plane(ta, 3, "ta3"))
         l6 = load_list(offs6, "l6")
         l7 = load_list(offs7, "l7")
+        sl_t = load_factors(nc.sync, sl, "sl_t")
+        sm_t = load_factors(nc.sync, sm, "sm_t")
         tl_t = [load_plane(tl, 0, "tl0")]
-        ta_t.append(load_plane(ta, 3, "ta3"))
         l3 = load_list(offs3, "l3")
         gb_t = load_factors(nc.sync, gb, "gb_t")
-        tl_t.append(load_plane(tl, 1, "tl1"))
-        l4 = load_list(offs4, "l4")
-        load_scale_rows(nc.sync, xo_sc, xo_scales, 0)
         xo_w = load_words(xo_words[0].rearrange("p n t -> p (n t)"), "xo_w")
+        l4 = load_list(offs4, "l4")
+        tl_t.append(load_plane(tl, 1, "tl1"))
         for t in range(2, PACK):
             tl_t.append(load_plane(tl, t, "tl%d" % t))
         l5 = load_list(offs5, "l5")
-        sa_t = load_factors(nc.sync, sa, "sa_t")
         wb_w = load_words(wb_words[0], "wb_w")
 
         w2_dealt = keep.tile([P, 2 * R], U8, align_bytes=64)
@@ -119,12 +119,13 @@ def tile_picked_codepage_plain_bank_codedbounds_one_plain_kernel(
             nc.vector.tensor_copy(pages[t][:].indirect(l2[:]), xcd[t][:])
             if t == 1:
                 nc.scalar.copy(
-                    w2_dealt[:].bitcast(U16).rearrange("p (t c i) -> p c t i", t=PACK, i=8),
-                    w2_raw[:].bitcast(U16).rearrange("p (c i t) -> p c t i", t=PACK, i=8),
+                    w2_dealt[:].bitcast(U16).rearrange("p (t m) -> p m t", t=PACK),
+                    w2_raw[:].bitcast(U16).rearrange("p (m t) -> p m t", t=PACK),
                 )
+            if t == 1:
                 nc.scalar.copy(
-                    w_dealt[:].rearrange("p (t c i) -> p c t i", t=PACK, i=4),
-                    w_raw[:].bitcast(U32).rearrange("p (c i t) -> p c t i", t=PACK, i=4),
+                    w_dealt[:].rearrange("p (t m) -> p m t", t=PACK),
+                    w_raw[:].bitcast(U32).rearrange("p (m t) -> p m t", t=PACK),
                 )
 
         upper = keep.tile([P, PACK, O], F32)
@@ -142,26 +143,30 @@ def tile_picked_codepage_plain_bank_codedbounds_one_plain_kernel(
 
         read_page(0)
         read_page(1)
-        bounds(1)
         read_page(2)
         read_page(3)
-        bounds(2)
-        bounds(3)
+        for t in range(1, PACK):
+            bounds(t)
 
         xo_gw = keep.tile([P, J], U32, align_bytes=64)
         xo_gs = keep.tile([P, J], U8, align_bytes=64)
-        nc.vector.tensor_copy(xo_gw[:], xo_w[:].bitcast(U32).indirect(l4[:]))
         nc.vector.tensor_copy(xo_gs[:], xo_sc[:].indirect(l4[:]))
+        nc.vector.tensor_copy(xo_gw[:], xo_w[:].bitcast(U32).indirect(l4[:]))
 
         xc_in = keep.tile([P, J, PACK], BF16, tag="xo_w", align_bytes=64)
-        nc.vector.tensor_copy(
-            xc_in[:].rearrange("p (c i) t -> p c t i", i=4),
-            xc_planes[:].rearrange("p t (c i) -> p c t i", i=4),
-        )
+        halves = [slice(0, J // 2), slice(J // 2, J)]
+        for js in halves:
+            nc.vector.tensor_copy(
+                xc_in[:, js, :].rearrange("p (c i) t -> p c t i", i=4),
+                xc_planes[:, :, js].rearrange("p t (c i) -> p c t i", i=4),
+            )
 
         xc_w = keep.tile([P, J], U32, align_bytes=64)
         xc_s = keep.tile([P, J], U8, align_bytes=64)
-        nc.vector.quantize_mx(out=xc_w[:].bitcast(FP8X4), scales=xc_s[:], in_=xc_in[:].rearrange("p j t -> p (j t)"))
+        for js in halves:
+            nc.vector.quantize_mx(
+                out=xc_w[:, js].bitcast(FP8X4), scales=xc_s[:, js], in_=xc_in[:, js, :].rearrange("p j t -> p (j t)")
+            )
 
         banks = [psum.tile([P, J], F32, name="bank%d" % t) for t in range(PACK)]
         for t in range(PACK):
@@ -192,17 +197,25 @@ def tile_picked_codepage_plain_bank_codedbounds_one_plain_kernel(
             nc.vector.tensor_copy(a_t[t][:], banks[t][:])
         for t in range(PACK):
             nc.scalar.activation(out=picked[:, t, :], in_=a_t[t][:].indirect(l5[:]), func=COPY, scale=sa_t[:, t : t + 1])
-            nc.vector.tensor_tensor(capped[:, t, :], picked[:, t, :], upper[:, t, :], ALU.min)
+        last = PACK - 1
+        places = [slice(0, O // 2), slice(O // 2, O)]
+        nc.vector.tensor_tensor(capped[:, 0:last, :], picked[:, 0:last, :], upper[:, 0:last, :], ALU.min)
+        for cols in places:
+            nc.vector.tensor_tensor(capped[:, last, cols], picked[:, last, cols], upper[:, last, cols], ALU.min)
         hid_in = keep.tile([P, O, PACK], BF16, align_bytes=64)
-        nc.vector.tensor_tensor(
-            hid_in[:].rearrange("p (c i) t -> p c t i", i=4),
-            capped[:].rearrange("p t (c i) -> p c t i", i=4),
-            lower[:].rearrange("p t (c i) -> p c t i", i=4),
-            ALU.max,
-        )
+        for cols in places:
+            nc.vector.tensor_tensor(
+                hid_in[:, cols, :].rearrange("p (c i) t -> p c t i", i=4),
+                capped[:, :, cols].rearrange("p t (c i) -> p c t i", i=4),
+                lower[:, :, cols].rearrange("p t (c i) -> p c t i", i=4),
+                ALU.max,
+            )
         hid_w = keep.tile([P, O], U32, align_bytes=64)
         hid_s = keep.tile([P, O], U8, align_bytes=64)
-        nc.vector.quantize_mx(out=hid_w[:].bitcast(FP8X4), scales=hid_s[:], in_=hid_in[:].rearrange("p o t -> p (o t)"))
+        for cols in places:
+            nc.vector.quantize_mx(
+                out=hid_w[:, cols].bitcast(FP8X4), scales=hid_s[:, cols], in_=hid_in[:, cols, :].rearrange("p o t -> p (o t)")
+            )
 
         wb_bytes = wb_w[:].bitcast(U8)
         for h in range(N // P):

@@ -69,15 +69,15 @@ def tile_picked_codepage_plain_bank_codedbounds_one_plain_kernel(
         warm = keep.tile([P, 2], F32)
         nc.vector.memset(warm[:, 0:1], 0.0)
         nc.scalar.activation(out=warm[:, 1:2], in_=warm[:, 0:1], func=COPY)
-        nc.gpsimd.memset(xo_sc[:].bitcast(I32), 0)
+        sl_t = load_factors(nc.gpsimd, sl, "sl_t")
+        sm_t = load_factors(nc.gpsimd, sm, "sm_t")
+        nc.vector.memset(xo_sc[:].bitcast(I32), 0)
         load_scale_rows(nc.gpsimd, xo_sc, xo_scales, 0)
-        nc.gpsimd.memset(wb_sc[:].bitcast(I32), 0)
         nc.vector.memset(spread[:], 0)
+        nc.vector.memset(wb_sc[:].bitcast(I32), 0)
         for t in range(PACK):
             nc.vector.memset(pages[t][:], 0.0)
 
-        sa_t = load_factors(nc.gpsimd, sa, "sa_t")
-        load_scale_rows(nc.gpsimd, wb_sc, wb_scales, 0)
         for q in range(4):
             nc.vector.tensor_copy(spread[QUAD * q : QUAD * q + 4, :], staged[:, q, :])
         sc_dealt = keep.tile([P, 2 * R], U8, align_bytes=64)
@@ -97,8 +97,6 @@ def tile_picked_codepage_plain_bank_codedbounds_one_plain_kernel(
         ta_t.append(load_plane(ta, 3, "ta3"))
         l6 = load_list(offs6, "l6")
         l7 = load_list(offs7, "l7")
-        sl_t = load_factors(nc.sync, sl, "sl_t")
-        sm_t = load_factors(nc.sync, sm, "sm_t")
         tl_t = [load_plane(tl, 0, "tl0")]
         l3 = load_list(offs3, "l3")
         gb_t = load_factors(nc.sync, gb, "gb_t")
@@ -108,7 +106,9 @@ def tile_picked_codepage_plain_bank_codedbounds_one_plain_kernel(
         for t in range(2, PACK):
             tl_t.append(load_plane(tl, t, "tl%d" % t))
         l5 = load_list(offs5, "l5")
+        sa_t = load_factors(nc.sync, sa, "sa_t")
         wb_w = load_words(wb_words[0], "wb_w")
+        load_scale_rows(nc.sync, wb_sc, wb_scales, 0)
 
         w2_dealt = keep.tile([P, 2 * R], U8, align_bytes=64)
         w_dealt = keep.tile([P, R], U32, align_bytes=64)
@@ -150,10 +150,10 @@ def tile_picked_codepage_plain_bank_codedbounds_one_plain_kernel(
 
         xo_gw = keep.tile([P, J], U32, align_bytes=64)
         xo_gs = keep.tile([P, J], U8, align_bytes=64)
-        nc.vector.tensor_copy(xo_gs[:], xo_sc[:].indirect(l4[:]))
         nc.vector.tensor_copy(xo_gw[:], xo_w[:].bitcast(U32).indirect(l4[:]))
+        nc.vector.tensor_copy(xo_gs[:], xo_sc[:].indirect(l4[:]))
 
-        xc_in = keep.tile([P, J, PACK], BF16, tag="xo_w", align_bytes=64)
+        xc_in = keep.tile([P, J, PACK], BF16, tag="xo_sc", align_bytes=64)
         halves = [slice(0, J // 2), slice(J // 2, J)]
         for js in halves:
             nc.vector.tensor_copy(

from contextlib import ExitStack

import concourse.mybir as mybir

K, J, R, T, U, Z, M, O, D, N = 512, 256, 512, 1024, 512, 512, 1024, 128, 512, 256
FLOPS = 2 * (K * R * J + Z * R * J + R * N * O)

F32 = mybir.dt.float32
BF16 = mybir.dt.bfloat16
I32 = mybir.dt.int32
U32 = mybir.dt.uint32
U16 = mybir.dt.uint16
U8 = mybir.dt.uint8
FP8X4 = mybir.dt.float8_e4m3fn_x4
FP4X4 = mybir.dt.float4_e2m1fn_x4
COPY = mybir.ActivationFunctionType.Copy
ALU = mybir.AluOpType

P = 128
PACK = 4
QUAD = 32


def tile_picked_codepage_plain_bank_codedbounds_one_plain_kernel(
    tc, ta, ga, gb, w_words, w_scales, xo_words, xo_scales, w2_words, w2_scales, tl, sa, sl, sm,
    wb_words, wb_scales, offs, offs2, offs3, offs4, offs5, offs6, offs7, out,
):
    nc = tc.nc
    with ExitStack() as ctx:
        keep = ctx.enter_context(tc.tile_pool(name="keep", bufs=1))
        psum = ctx.enter_context(tc.psum_pool(name="psum", bufs=1))

        def load_list(src, name):
            tile = keep.tile(list(src.shape), U16, name=name)
            nc.sync.dma_start(tile[:], src)
            return tile

        def load_factors(queue, src, name):
            tile = keep.tile([P, PACK], F32, name=name)
            queue.dma_start(tile[:], src.rearrange("(p t) o -> p (t o)", t=PACK))
            return tile

        def load_plane(src, t, name):
            tile = keep.tile([P, src.shape[1]], F32, name=name, align_bytes=64)
            nc.sync.dma_start(tile[:], src.rearrange("(p t) c -> p t c", t=PACK)[:, t, :])
            return tile

        def load_words(src, name):
            words = src.bitcast(I32)
            tile = keep.tile([P, words.shape[1]], I32, name=name, align_bytes=64)
            nc.sync.dma_start(tile[:], words)
            return tile

        def load_scale_rows(queue, tile, src, first):
            rows = src[0].bitcast(I32)
            for q in range(4):
                p0 = QUAD * q + first
                queue.dma_start(tile[p0 : p0 + 4, :].bitcast(I32), rows[4 * q : 4 * q + 4, :])

        pages = [keep.tile([P, U], F32, name="page%d" % t) for t in range(PACK)]
        xo_sc = keep.tile([P, M], U8, align_bytes=64)
        RW = R // 4
        spread = keep.tile([P, 2 * RW], I32, align_bytes=64)
        wb_sc = keep.tile([P, N], U8, align_bytes=64)
        staged = keep.tile([PACK, PACK, 2 * RW], I32)
        for src, c0 in ((w2_scales, 0), (w_scales, RW)):
            rows = src[0].bitcast(I32).rearrange("(q i) c -> i q c", i=PACK)
            nc.sync.dma_start(staged[:, :, c0 : c0 + RW], rows)
        warm = keep.tile([P, 2], F32)
        nc.vector.memset(warm[:, 0:1], 0.0)
        nc.scalar.activation(out=warm[:, 1:2], in_=warm[:, 0:1], func=COPY)
        sl_t = load_factors(nc.gpsimd, sl, "sl_t")
        sm_t = load_factors(nc.gpsimd, sm, "sm_t")
        nc.vector.memset(xo_sc[:].bitcast(I32), 0)
        load_scale_rows(nc.gpsimd, xo_sc, xo_scales, 0)
        nc.vector.memset(spread[:], 0)
        nc.vector.memset(wb_sc[:].bitcast(I32), 0)
        for t in range(PACK):
            nc.vector.memset(pages[t][:], 0.0)

        for q in range(4):
            nc.vector.tensor_copy(spread[QUAD * q : QUAD * q + 4, :], staged[:, q, :])
        sc_dealt = keep.tile([P, 2 * R], U8, align_bytes=64)
        nc.vector.tensor_copy(
            sc_dealt[:].rearrange("p (w t c i) -> p w c t i", w=2, t=PACK, i=16),
            spread[:].bitcast(U8).rearrange("p (w c i t) -> p w c t i", w=2, t=PACK, i=16),
        )

        ta_t = [load_plane(ta, 0, "ta0")]
        l1 = load_list(offs, "l1")
        ga_t = load_factors(nc.sync, ga, "ga_t")
        l2 = load_list(offs2, "l2")
        ta_t.append(load_plane(ta, 1, "ta1"))
        w2_raw = load_words(w2_words[0], "w2_raw")
        w_raw = load_words(w_words[0].rearrange("p n t -> p (n t)"), "w_raw")
        ta_t.append(load_plane(ta, 2, "ta2"))
        ta_t.append(load_plane(ta, 3, "ta3"))
        l6 = load_list(offs6, "l6")
        l7 = load_list(offs7, "l7")
        tl_t = [load_plane(tl, 0, "tl0")]
        l3 = load_list(offs3, "l3")
        gb_t = load_factors(nc.sync, gb, "gb_t")
        xo_w = load_words(xo_words[0].rearrange("p n t -> p (n t)"), "xo_w")
        l4 = load_list(offs4, "l4")
        tl_t.append(load_plane(tl, 1, "tl1"))
        for t in range(2, PACK):
            tl_t.append(load_plane(tl, t, "tl%d" % t))
        l5 = load_list(offs5, "l5")
        sa_t = load_factors(nc.sync, sa, "sa_t")
        wb_w = load_words(wb_words[0], "wb_w")
        load_scale_rows(nc.sync, wb_sc, wb_scales, 0)

        w2_dealt = keep.tile([P, 2 * R], U8, align_bytes=64)
        w_dealt = keep.tile([P, R], U32, align_bytes=64)

        xcd = [keep.tile([P, J], F32, name="xcd%d" % t) for t in range(PACK)]
        for t in range(PACK):
            nc.scalar.activation(out=xcd[t][:], in_=ta_t[t][:].indirect(l1[:]), func=COPY, scale=ga_t[:, t : t + 1])
            nc.vector.tensor_copy(pages[t][:].indirect(l2[:]), xcd[t][:])
            if t == 1:
                nc.scalar.copy(
                    w2_dealt[:].bitcast(U16).rearrange("p (t m) -> p m t", t=PACK),
                    w2_raw[:].bitcast(U16).rearrange("p (m t) -> p m t", t=PACK),
                )
            if t == 1:
                nc.scalar.copy(
                    w_dealt[:].rearrange("p (t m) -> p m t", t=PACK),
                    w_raw[:].bitcast(U32).rearrange("p (m t) -> p m t", t=PACK),
                )

        upper = keep.tile([P, PACK, O], F32)
        lower = keep.tile([P, PACK, O], F32)

        def bounds(t):
            nc.scalar.activation(out=upper[:, t, :], in_=tl_t[t][:].indirect(l6[:]), func=COPY, scale=sl_t[:, t : t + 1])
            nc.scalar.activation(out=lower[:, t, :], in_=tl_t[t][:].indirect(l7[:]), func=COPY, scale=sm_t[:, t : t + 1])

        bounds(0)
        xc_planes = keep.tile([P, PACK, J], BF16, tag="ta3", align_bytes=64)

        def read_page(t):
            nc.scalar.activation(out=xc_planes[:, t, :], in_=pages[t][:].indirect(l3[:]), func=COPY, scale=gb_t[:, t : t + 1])

        read_page(0)
        read_page(1)
        read_page(2)
        read_page(3)
        for t in range(1, PACK):
            bounds(t)

        xo_gw = keep.tile([P, J], U32, align_bytes=64)
        xo_gs = keep.tile([P, J], U8, align_bytes=64)
        nc.vector.tensor_copy(xo_gw[:], xo_w[:].bitcast(U32).indirect(l4[:]))
        nc.vector.tensor_copy(xo_gs[:], xo_sc[:].indirect(l4[:]))

        xc_in = keep.tile([P, J, PACK], BF16, tag="xo_sc", align_bytes=64)
        halves = [slice(0, J // 2), slice(J // 2, J)]
        for js in halves:
            nc.vector.tensor_copy(
                xc_in[:, js, :].rearrange("p (c i) t -> p c t i", i=4),
                xc_planes[:, :, js].rearrange("p t (c i) -> p c t i", i=4),
            )

        xc_w = keep.tile([P, J], U32, align_bytes=64)
        xc_s = keep.tile([P, J], U8, align_bytes=64)
        for js in halves:
            nc.vector.quantize_mx(
                out=xc_w[:, js].bitcast(FP8X4), scales=xc_s[:, js], in_=xc_in[:, js, :].rearrange("p j t -> p (j t)")
            )

        banks = [psum.tile([P, J], F32, name="bank%d" % t) for t in range(PACK)]
        for t in range(PACK):
            nc.tensor.matmul_mx(
                out=banks[t][:],
                lhsT=w2_dealt[:, 2 * P * t : 2 * P * (t + 1)].bitcast(FP4X4),
                lhsT_scale=sc_dealt[:, P * t : P * (t + 1)],
                rhs=xo_gw[:].bitcast(FP8X4),
                rhs_scale=xo_gs[:],
                start=True,
                stop=False,
            )
        for t in range(PACK):
            nc.tensor.matmul_mx(
                out=banks[t][:],
                lhsT=w_dealt[:, P * t : P * (t + 1)].bitcast(FP8X4),
                lhsT_scale=sc_dealt[:, R + P * t : R + P * (t + 1)],
                rhs=xc_w[:].bitcast(FP8X4),
                rhs_scale=xc_s[:],
                start=False,
                stop=True,
            )

        a_t = [keep.tile([P, J], F32, name="a%d" % t) for t in range(PACK)]
        picked = keep.tile([P, PACK, O], F32)
        capped = keep.tile([P, PACK, O], F32)
        for t in range(PACK):
            nc.vector.tensor_copy(a_t[t][:], banks[t][:])
        for t in range(PACK):
            nc.scalar.activation(out=picked[:, t, :], in_=a_t[t][:].indirect(l5[:]), func=COPY, scale=sa_t[:, t : t + 1])
        last = PACK - 1
        places = [slice(0, O // 2), slice(O // 2, O)]
        nc.vector.tensor_tensor(capped[:, 0:last, :], picked[:, 0:last, :], upper[:, 0:last, :], ALU.min)
        for cols in places:
            nc.vector.tensor_tensor(capped[:, last, cols], picked[:, last, cols], upper[:, last, cols], ALU.min)
        hid_in = keep.tile([P, O, PACK], BF16, align_bytes=64)
        for cols in places:
            nc.vector.tensor_tensor(
                hid_in[:, cols, :].rearrange("p (c i) t -> p c t i", i=4),
                capped[:, :, cols].rearrange("p t (c i) -> p c t i", i=4),
                lower[:, :, cols].rearrange("p t (c i) -> p c t i", i=4),
                ALU.max,
            )
        hid_w = keep.tile([P, O], U32, align_bytes=64)
        hid_s = keep.tile([P, O], U8, align_bytes=64)
        for cols in places:
            nc.vector.quantize_mx(
                out=hid_w[:, cols].bitcast(FP8X4), scales=hid_s[:, cols], in_=hid_in[:, cols, :].rearrange("p o t -> p (o t)")
            )

        wb_bytes = wb_w[:].bitcast(U8)
        for h in range(N // P):
            acc = psum.tile([P, O], F32, name="acc%d" % h)
            nc.tensor.matmul_mx(
                out=acc[:],
                lhsT=wb_bytes[:, 2 * P * h : 2 * P * (h + 1)].bitcast(FP4X4),
                lhsT_scale=wb_sc[:, P * h : P * (h + 1)],
                rhs=hid_w[:].bitcast(FP8X4),
                rhs_scale=hid_s[:],
                start=True,
                stop=True,
            )
            res = keep.tile([P, O], F32, name="res%d" % h)
            if h == 0:
                nc.vector.tensor_copy(res[:], acc[:])
                nc.sync.dma_start(out[P * h : P * (h + 1), :], res[:])
            else:
                nc.scalar.copy(res[:], acc[:])
                nc.scalar.dma_start(out[P * h : P * (h + 1), :], res[:])
